import numpy as np
import ml_dtypes

BF16 = ml_dtypes.bfloat16


def bf(x):
    return np.asarray(x, np.float32).astype(BF16)


def f32(x):
    return np.asarray(x, np.float32)


def f64(x):
    return np.asarray(x).astype(np.float64)


def striped(idx):
    return np.tile(idx.reshape(-1, 16).T, (8, 1))


S, K, M, N, H = 1024, 256, 256, 256, 128


def sigmoid(v):
    return 1.0 / (1.0 + np.exp(-v))


def setup_inputs():
    return {"table": bf(np.random.standard_normal((K, S))), "w": bf(np.random.standard_normal((K, M)) / np.sqrt(K)), "offs": striped(np.random.permutation(np.tile(np.arange(S), 2))[:N])}


def reference(table, w, offs):
    idx = offs[:16].T.reshape(-1)
    x = f64(table)[:, idx]
    y = f64(w).T @ x
    return y[:H] * sigmoid(y[H:])

@@ -1,0 +1,43 @@
+import concourse.mybir as mybir
+
+BF16, F32, U16 = mybir.dt.bfloat16, mybir.dt.float32, mybir.dt.uint16
+
+P = 128
+K, S = 256, 1024
+M, N = 256, 256
+H = M // 2
+K_BLOCKS = K // P
+
+FLOPS = 2 * K * M * N
+
+
+def tile_gather_matmul_kernel(tc, table, w, offs, out):
+    nc = tc.nc
+    with (
+        tc.tile_pool(name="held", bufs=1) as held,
+        tc.psum_pool(name="banks", bufs=1) as banks,
+    ):
+        offsets = held.tile([P, N // 16], U16, name="offsets")
+        nc.sync.dma_start(offsets[:], offs)
+
+        queues = (nc.sync, nc.scalar)
+        w_blocks = [held.tile([P, M], BF16, name="w%d" % b) for b in range(K_BLOCKS)]
+        table_blocks = [held.tile([P, S], BF16, name="table%d" % b) for b in range(K_BLOCKS)]
+        for b in range(K_BLOCKS):
+            queues[b].dma_start(w_blocks[b][:], w[b * P : (b + 1) * P, :])
+        for b in range(K_BLOCKS):
+            queues[b].dma_start(table_blocks[b][:], table[b * P : (b + 1) * P, :])
+
+        y_gate = banks.tile([P, N], F32, name="y_gate")
+        y_value = banks.tile([P, N], F32, name="y_value")
+        for b in range(K_BLOCKS):
+            picked = table_blocks[b][:].indirect(offsets[:])
+            first, last = b == 0, b == K_BLOCKS - 1
+            nc.tensor.matmul(y_gate[:], w_blocks[b][:, H:M], picked, start=first, stop=last)
+            nc.tensor.matmul(y_value[:], w_blocks[b][:, 0:H], picked, start=first, stop=last)
+
+        gate = held.tile([P, N], F32, name="gate")
+        nc.scalar.activation(gate[:], y_gate[:], mybir.ActivationFunctionType.Sigmoid)
+        gated = held.tile([P, N], F32, name="gated")
+        nc.vector.tensor_tensor(gated[:], y_value[:], gate[:], mybir.AluOpType.mult)
+        nc.sync.dma_start(out, gated[:])

@@ -20,13 +20,11 @@ def tile_gather_matmul_kernel(tc, table, w, offs, out):
         offsets = held.tile([P, N // 16], U16, name="offsets")
         nc.sync.dma_start(offsets[:], offs)
 
-        queues = (nc.sync, nc.scalar)
         w_blocks = [held.tile([P, M], BF16, name="w%d" % b) for b in range(K_BLOCKS)]
         table_blocks = [held.tile([P, S], BF16, name="table%d" % b) for b in range(K_BLOCKS)]
         for b in range(K_BLOCKS):
-            queues[b].dma_start(w_blocks[b][:], w[b * P : (b + 1) * P, :])
-        for b in range(K_BLOCKS):
-            queues[b].dma_start(table_blocks[b][:], table[b * P : (b + 1) * P, :])
+            nc.sync.dma_start(w_blocks[b][:], w[b * P : (b + 1) * P, :])
+            nc.sync.dma_start(table_blocks[b][:], table[b * P : (b + 1) * P, :])
 
         y_gate = banks.tile([P, N], F32, name="y_gate")
         y_value = banks.tile([P, N], F32, name="y_value")

@@ -8,6 +8,8 @@ M, N = 256, 256
 H = M // 2
 K_BLOCKS = K // P
 
+WARM_MATMULS = 16
+
 FLOPS = 2 * K * M * N
 
 
@@ -25,6 +27,12 @@ def tile_gather_matmul_kernel(tc, table, w, offs, out):
         for b in range(K_BLOCKS):
             nc.sync.dma_start(w_blocks[b][:], w[b * P : (b + 1) * P, :])
             nc.sync.dma_start(table_blocks[b][:], table[b * P : (b + 1) * P, :])
+
+        zeros = held.tile([P, P], BF16, name="zeros")
+        nc.vector.memset(zeros[:], 0.0)
+        idle_bank = banks.tile([P, P], F32, name="idle_bank")
+        for i in range(WARM_MATMULS):
+            nc.tensor.matmul(idle_bank[:], zeros[:], zeros[:], start=True, stop=True)
 
         y_gate = banks.tile([P, N], F32, name="y_gate")
         y_value = banks.tile([P, N], F32, name="y_value")

@@ -7,8 +7,8 @@ K, S = 256, 1024
 M, N = 256, 256
 H = M // 2
 K_BLOCKS = K // P
-
-WARM_MATMULS = 16
+PIECES = 2
+Q = N // PIECES
 
 FLOPS = 2 * K * M * N
 
@@ -17,6 +17,7 @@ def tile_gather_matmul_kernel(tc, table, w, offs, out):
     nc = tc.nc
     with (
         tc.tile_pool(name="held", bufs=1) as held,
+        tc.tile_pool(name="work", bufs=PIECES) as work,
         tc.psum_pool(name="banks", bufs=1) as banks,
     ):
         offsets = held.tile([P, N // 16], U16, name="offsets")
@@ -28,22 +29,18 @@ def tile_gather_matmul_kernel(tc, table, w, offs, out):
             nc.sync.dma_start(w_blocks[b][:], w[b * P : (b + 1) * P, :])
             nc.sync.dma_start(table_blocks[b][:], table[b * P : (b + 1) * P, :])
 
-        zeros = held.tile([P, P], BF16, name="zeros")
-        nc.vector.memset(zeros[:], 0.0)
-        idle_bank = banks.tile([P, P], F32, name="idle_bank")
-        for i in range(WARM_MATMULS):
-            nc.tensor.matmul(idle_bank[:], zeros[:], zeros[:], start=True, stop=True)
-
-        y_gate = banks.tile([P, N], F32, name="y_gate")
-        y_value = banks.tile([P, N], F32, name="y_value")
+        y_gate = [banks.tile([P, Q], F32, name="y_gate%d" % c) for c in range(PIECES)]
+        y_value = [banks.tile([P, Q], F32, name="y_value%d" % c) for c in range(PIECES)]
         for b in range(K_BLOCKS):
-            picked = table_blocks[b][:].indirect(offsets[:])
             first, last = b == 0, b == K_BLOCKS - 1
-            nc.tensor.matmul(y_gate[:], w_blocks[b][:, H:M], picked, start=first, stop=last)
-            nc.tensor.matmul(y_value[:], w_blocks[b][:, 0:H], picked, start=first, stop=last)
+            for y, w_columns in ((y_gate, slice(H, M)), (y_value, slice(0, H))):
+                for c in range(PIECES):
+                    picked = table_blocks[b][:].indirect(offsets[:, c * (Q // 16) : (c + 1) * (Q // 16)])
+                    nc.tensor.matmul(y[c][:], w_blocks[b][:, w_columns], picked, start=first, stop=last)
 
-        gate = held.tile([P, N], F32, name="gate")
-        nc.scalar.activation(gate[:], y_gate[:], mybir.ActivationFunctionType.Sigmoid)
-        gated = held.tile([P, N], F32, name="gated")
-        nc.vector.tensor_tensor(gated[:], y_value[:], gate[:], mybir.AluOpType.mult)
-        nc.sync.dma_start(out, gated[:])
+        for c in range(PIECES):
+            gate = work.tile([P, Q], F32, name="gate")
+            nc.scalar.activation(gate[:], y_gate[c][:], mybir.ActivationFunctionType.Sigmoid)
+            gated = work.tile([P, Q], F32, name="gated")
+            nc.vector.tensor_tensor(gated[:], y_value[c][:], gate[:], mybir.AluOpType.mult)
+            nc.sync.dma_start(out[:, c * Q : (c + 1) * Q], gated[:])

@@ -7,8 +7,6 @@ K, S = 256, 1024
 M, N = 256, 256
 H = M // 2
 K_BLOCKS = K // P
-PIECES = 2
-Q = N // PIECES
 
 FLOPS = 2 * K * M * N
 
@@ -17,7 +15,6 @@ def tile_gather_matmul_kernel(tc, table, w, offs, out):
     nc = tc.nc
     with (
         tc.tile_pool(name="held", bufs=1) as held,
-        tc.tile_pool(name="work", bufs=PIECES) as work,
         tc.psum_pool(name="banks", bufs=1) as banks,
     ):
         offsets = held.tile([P, N // 16], U16, name="offsets")
@@ -27,20 +24,18 @@ def tile_gather_matmul_kernel(tc, table, w, offs, out):
         table_blocks = [held.tile([P, S], BF16, name="table%d" % b) for b in range(K_BLOCKS)]
         for b in range(K_BLOCKS):
             nc.sync.dma_start(w_blocks[b][:], w[b * P : (b + 1) * P, :])
-            nc.sync.dma_start(table_blocks[b][:], table[b * P : (b + 1) * P, :])
+            nc.scalar.dma_start(table_blocks[b][:], table[b * P : (b + 1) * P, :])
 
-        y_gate = [banks.tile([P, Q], F32, name="y_gate%d" % c) for c in range(PIECES)]
-        y_value = [banks.tile([P, Q], F32, name="y_value%d" % c) for c in range(PIECES)]
+        y_gate = banks.tile([P, N], F32, name="y_gate")
+        y_value = banks.tile([P, N], F32, name="y_value")
         for b in range(K_BLOCKS):
+            picked = table_blocks[b][:].indirect(offsets[:])
             first, last = b == 0, b == K_BLOCKS - 1
-            for y, w_columns in ((y_gate, slice(H, M)), (y_value, slice(0, H))):
-                for c in range(PIECES):
-                    picked = table_blocks[b][:].indirect(offsets[:, c * (Q // 16) : (c + 1) * (Q // 16)])
-                    nc.tensor.matmul(y[c][:], w_blocks[b][:, w_columns], picked, start=first, stop=last)
+            nc.tensor.matmul(y_gate[:], w_blocks[b][:, H:M], picked, start=first, stop=last)
+            nc.tensor.matmul(y_value[:], w_blocks[b][:, 0:H], picked, start=first, stop=last)
 
-        for c in range(PIECES):
-            gate = work.tile([P, Q], F32, name="gate")
-            nc.scalar.activation(gate[:], y_gate[c][:], mybir.ActivationFunctionType.Sigmoid)
-            gated = work.tile([P, Q], F32, name="gated")
-            nc.vector.tensor_tensor(gated[:], y_value[c][:], gate[:], mybir.AluOpType.mult)
-            nc.sync.dma_start(out[:, c * Q : (c + 1) * Q], gated[:])
+        gate = held.tile([P, N], F32, name="gate")
+        nc.scalar.activation(gate[:], y_gate[:], mybir.ActivationFunctionType.Sigmoid)
+        gated = held.tile([P, N], F32, name="gated")
+        nc.vector.tensor_tensor(gated[:], y_value[:], gate[:], mybir.AluOpType.mult)
+        nc.sync.dma_start(out, gated[:])

@@ -18,13 +18,14 @@ def tile_gather_matmul_kernel(tc, table, w, offs, out):
         tc.psum_pool(name="banks", bufs=1) as banks,
     ):
         offsets = held.tile([P, N // 16], U16, name="offsets")
-        nc.sync.dma_start(offsets[:], offs)
-
         w_blocks = [held.tile([P, M], BF16, name="w%d" % b) for b in range(K_BLOCKS)]
         table_blocks = [held.tile([P, S], BF16, name="table%d" % b) for b in range(K_BLOCKS)]
+
+        nc.sync.dma_start(table_blocks[0][:], table[0:P, :])
+        nc.sync.dma_start(offsets[:], offs)
+        nc.sync.dma_start(table_blocks[1][:], table[P : 2 * P, :])
         for b in range(K_BLOCKS):
-            nc.sync.dma_start(w_blocks[b][:], w[b * P : (b + 1) * P, :])
-            nc.scalar.dma_start(table_blocks[b][:], table[b * P : (b + 1) * P, :])
+            nc.scalar.dma_start(w_blocks[b][:], w[b * P : (b + 1) * P, :])
 
         y_gate = banks.tile([P, N], F32, name="y_gate")
         y_value = banks.tile([P, N], F32, name="y_value")

@@ -7,6 +7,7 @@ K, S = 256, 1024
 M, N = 256, 256
 H = M // 2
 K_BLOCKS = K // P
+DMA_ALIGN = 256
 
 FLOPS = 2 * K * M * N
 
@@ -18,8 +19,8 @@ def tile_gather_matmul_kernel(tc, table, w, offs, out):
         tc.psum_pool(name="banks", bufs=1) as banks,
     ):
         offsets = held.tile([P, N // 16], U16, name="offsets")
-        w_blocks = [held.tile([P, M], BF16, name="w%d" % b) for b in range(K_BLOCKS)]
-        table_blocks = [held.tile([P, S], BF16, name="table%d" % b) for b in range(K_BLOCKS)]
+        w_blocks = [held.tile([P, M], BF16, name="w%d" % b, align_bytes=DMA_ALIGN) for b in range(K_BLOCKS)]
+        table_blocks = [held.tile([P, S], BF16, name="table%d" % b, align_bytes=DMA_ALIGN) for b in range(K_BLOCKS)]
 
         nc.sync.dma_start(table_blocks[0][:], table[0:P, :])
         nc.sync.dma_start(offsets[:], offs)
@@ -37,6 +38,6 @@ def tile_gather_matmul_kernel(tc, table, w, offs, out):
 
         gate = held.tile([P, N], F32, name="gate")
         nc.scalar.activation(gate[:], y_gate[:], mybir.ActivationFunctionType.Sigmoid)
-        gated = held.tile([P, N], F32, name="gated")
+        gated = held.tile([P, N], F32, name="gated", align_bytes=DMA_ALIGN)
         nc.vector.tensor_tensor(gated[:], y_value[:], gate[:], mybir.AluOpType.mult)
         nc.sync.dma_start(out, gated[:])

@@ -7,6 +7,7 @@ K, S = 256, 1024
 M, N = 256, 256
 H = M // 2
 K_BLOCKS = K // P
+PIECE = N // 2
 DMA_ALIGN = 256
 
 FLOPS = 2 * K * M * N
@@ -37,7 +38,9 @@ def tile_gather_matmul_kernel(tc, table, w, offs, out):
             nc.tensor.matmul(y_value[:], w_blocks[b][:, 0:H], picked, start=first, stop=last)
 
         gate = held.tile([P, N], F32, name="gate")
-        nc.scalar.activation(gate[:], y_gate[:], mybir.ActivationFunctionType.Sigmoid)
         gated = held.tile([P, N], F32, name="gated", align_bytes=DMA_ALIGN)
-        nc.vector.tensor_tensor(gated[:], y_value[:], gate[:], mybir.AluOpType.mult)
+        for c in range(0, N, PIECE):
+            piece = slice(c, c + PIECE)
+            nc.scalar.activation(gate[:, piece], y_gate[:, piece], mybir.ActivationFunctionType.Sigmoid)
+            nc.vector.tensor_tensor(gated[:, piece], y_value[:, piece], gate[:, piece], mybir.AluOpType.mult)
         nc.sync.dma_start(out, gated[:])

@@ -20,22 +20,24 @@ def tile_gather_matmul_kernel(tc, table, w, offs, out):
         tc.psum_pool(name="banks", bufs=1) as banks,
     ):
         offsets = held.tile([P, N // 16], U16, name="offsets")
-        w_blocks = [held.tile([P, M], BF16, name="w%d" % b, align_bytes=DMA_ALIGN) for b in range(K_BLOCKS)]
+        w_all = held.tile([P, K_BLOCKS * M], BF16, name="w_all", align_bytes=DMA_ALIGN)
         table_blocks = [held.tile([P, S], BF16, name="table%d" % b, align_bytes=DMA_ALIGN) for b in range(K_BLOCKS)]
 
-        nc.sync.dma_start(table_blocks[0][:], table[0:P, :])
+        table_rows = table.rearrange("(p b) s -> p b s", b=K_BLOCKS)
+        nc.sync.dma_start(table_blocks[0][:], table_rows[:, 0, :])
         nc.sync.dma_start(offsets[:], offs)
-        nc.sync.dma_start(table_blocks[1][:], table[P : 2 * P, :])
-        for b in range(K_BLOCKS):
-            nc.scalar.dma_start(w_blocks[b][:], w[b * P : (b + 1) * P, :])
+        nc.sync.dma_start(table_blocks[1][:], table_rows[:, 1, :])
+        nc.scalar.dma_start(w_all[:], w.rearrange("(p b) m -> p (b m)", b=K_BLOCKS))
 
         y_gate = banks.tile([P, N], F32, name="y_gate")
         y_value = banks.tile([P, N], F32, name="y_value")
         for b in range(K_BLOCKS):
             picked = table_blocks[b][:].indirect(offsets[:])
             first, last = b == 0, b == K_BLOCKS - 1
-            nc.tensor.matmul(y_gate[:], w_blocks[b][:, H:M], picked, start=first, stop=last)
-            nc.tensor.matmul(y_value[:], w_blocks[b][:, 0:H], picked, start=first, stop=last)
+            w_value = w_all[:, b * M : b * M + H]
+            w_gate = w_all[:, b * M + H : (b + 1) * M]
+            nc.tensor.matmul(y_gate[:], w_gate, picked, start=first, stop=last)
+            nc.tensor.matmul(y_value[:], w_value, picked, start=first, stop=last)
 
         gate = held.tile([P, N], F32, name="gate")
         gated = held.tile([P, N], F32, name="gated", align_bytes=DMA_ALIGN)

@@ -7,7 +7,8 @@ K, S = 256, 1024
 M, N = 256, 256
 H = M // 2
 K_BLOCKS = K // P
-PIECE = N // 2
+PIECES = 2
+PIECE = N // PIECES
 DMA_ALIGN = 256
 
 FLOPS = 2 * K * M * N
@@ -29,20 +30,22 @@ def tile_gather_matmul_kernel(tc, table, w, offs, out):
         nc.sync.dma_start(table_blocks[1][:], table_rows[:, 1, :])
         nc.scalar.dma_start(w_all[:], w.rearrange("(p b) m -> p (b m)", b=K_BLOCKS))
 
-        y_gate = banks.tile([P, N], F32, name="y_gate")
+        y_gates = [banks.tile([P, PIECE], F32, name="y_gate%d" % i) for i in range(PIECES)]
         y_value = banks.tile([P, N], F32, name="y_value")
         for b in range(K_BLOCKS):
-            picked = table_blocks[b][:].indirect(offsets[:])
+            words = table_blocks[b][:]
             first, last = b == 0, b == K_BLOCKS - 1
             w_value = w_all[:, b * M : b * M + H]
             w_gate = w_all[:, b * M + H : (b + 1) * M]
-            nc.tensor.matmul(y_gate[:], w_gate, picked, start=first, stop=last)
-            nc.tensor.matmul(y_value[:], w_value, picked, start=first, stop=last)
+            for i in range(PIECES):
+                piece_of_list = offsets[:, i * (PIECE // 16) : (i + 1) * (PIECE // 16)]
+                nc.tensor.matmul(y_gates[i][:], w_gate, words.indirect(piece_of_list), start=first, stop=last)
+            nc.tensor.matmul(y_value[:], w_value, words.indirect(offsets[:]), start=first, stop=last)
 
         gate = held.tile([P, N], F32, name="gate")
         gated = held.tile([P, N], F32, name="gated", align_bytes=DMA_ALIGN)
-        for c in range(0, N, PIECE):
-            piece = slice(c, c + PIECE)
-            nc.scalar.activation(gate[:, piece], y_gate[:, piece], mybir.ActivationFunctionType.Sigmoid)
+        for i in range(PIECES):
+            piece = slice(i * PIECE, (i + 1) * PIECE)
+            nc.scalar.activation(gate[:, piece], y_gates[i][:], mybir.ActivationFunctionType.Sigmoid)
             nc.vector.tensor_tensor(gated[:, piece], y_value[:, piece], gate[:, piece], mybir.AluOpType.mult)
         nc.sync.dma_start(out, gated[:])

@@ -31,21 +31,20 @@ def tile_gather_matmul_kernel(tc, table, w, offs, out):
         nc.scalar.dma_start(w_all[:], w.rearrange("(p b) m -> p (b m)", b=K_BLOCKS))
 
         y_gates = [banks.tile([P, PIECE], F32, name="y_gate%d" % i) for i in range(PIECES)]
-        y_value = banks.tile([P, N], F32, name="y_value")
+        y_values = [banks.tile([P, PIECE], F32, name="y_value%d" % i) for i in range(PIECES)]
         for b in range(K_BLOCKS):
-            words = table_blocks[b][:]
             first, last = b == 0, b == K_BLOCKS - 1
             w_value = w_all[:, b * M : b * M + H]
             w_gate = w_all[:, b * M + H : (b + 1) * M]
-            for i in range(PIECES):
-                piece_of_list = offsets[:, i * (PIECE // 16) : (i + 1) * (PIECE // 16)]
-                nc.tensor.matmul(y_gates[i][:], w_gate, words.indirect(piece_of_list), start=first, stop=last)
-            nc.tensor.matmul(y_value[:], w_value, words.indirect(offsets[:]), start=first, stop=last)
+            for y_pieces, weights in ((y_gates, w_gate), (y_values, w_value)):
+                for i in range(PIECES):
+                    picked = table_blocks[b][:].indirect(offsets[:, i * (PIECE // 16) : (i + 1) * (PIECE // 16)])
+                    nc.tensor.matmul(y_pieces[i][:], weights, picked, start=first, stop=last)
 
         gate = held.tile([P, N], F32, name="gate")
         gated = held.tile([P, N], F32, name="gated", align_bytes=DMA_ALIGN)
         for i in range(PIECES):
             piece = slice(i * PIECE, (i + 1) * PIECE)
             nc.scalar.activation(gate[:, piece], y_gates[i][:], mybir.ActivationFunctionType.Sigmoid)
-            nc.vector.tensor_tensor(gated[:, piece], y_value[:, piece], gate[:, piece], mybir.AluOpType.mult)
+            nc.vector.tensor_tensor(gated[:, piece], y_values[i][:], gate[:, piece], mybir.AluOpType.mult)
         nc.sync.dma_start(out, gated[:])

import concourse.mybir as mybir

BF16, F32, U16 = mybir.dt.bfloat16, mybir.dt.float32, mybir.dt.uint16

P = 128
K, S = 256, 1024
M, N = 256, 256
H = M // 2
K_BLOCKS = K // P
PIECES = 2
PIECE = N // PIECES
DMA_ALIGN = 256

FLOPS = 2 * K * M * N


def tile_gather_matmul_kernel(tc, table, w, offs, out):
    nc = tc.nc
    with (
        tc.tile_pool(name="held", bufs=1) as held,
        tc.psum_pool(name="banks", bufs=1) as banks,
    ):
        offsets = held.tile([P, N // 16], U16, name="offsets")
        w_all = held.tile([P, K_BLOCKS * M], BF16, name="w_all", align_bytes=DMA_ALIGN)
        table_blocks = [held.tile([P, S], BF16, name="table%d" % b, align_bytes=DMA_ALIGN) for b in range(K_BLOCKS)]

        table_rows = table.rearrange("(p b) s -> p b s", b=K_BLOCKS)
        nc.sync.dma_start(table_blocks[0][:], table_rows[:, 0, :])
        nc.sync.dma_start(offsets[:], offs)
        nc.sync.dma_start(table_blocks[1][:], table_rows[:, 1, :])
        nc.scalar.dma_start(w_all[:], w.rearrange("(p b) m -> p (b m)", b=K_BLOCKS))

        y_gates = [banks.tile([P, PIECE], F32, name="y_gate%d" % i) for i in range(PIECES)]
        y_values = [banks.tile([P, PIECE], F32, name="y_value%d" % i) for i in range(PIECES)]
        for b in range(K_BLOCKS):
            first, last = b == 0, b == K_BLOCKS - 1
            w_value = w_all[:, b * M : b * M + H]
            w_gate = w_all[:, b * M + H : (b + 1) * M]
            for y_pieces, weights in ((y_gates, w_gate), (y_values, w_value)):
                for i in range(PIECES):
                    picked = table_blocks[b][:].indirect(offsets[:, i * (PIECE // 16) : (i + 1) * (PIECE // 16)])
                    nc.tensor.matmul(y_pieces[i][:], weights, picked, start=first, stop=last)

        gate = held.tile([P, N], F32, name="gate")
        gated = held.tile([P, N], F32, name="gated", align_bytes=DMA_ALIGN)
        for i in range(PIECES):
            piece = slice(i * PIECE, (i + 1) * PIECE)
            nc.scalar.activation(gate[:, piece], y_gates[i][:], mybir.ActivationFunctionType.Sigmoid)
            nc.vector.tensor_tensor(gated[:, piece], y_values[i][:], gate[:, piece], mybir.AluOpType.mult)
        nc.sync.dma_start(out, gated[:])
